import numpy as np
CORES = [16,32,48,64,80]
N = 5
C, TIMES = 256, 1
def setup_inputs(rng):
    return {"x": np.exp(rng.standard_normal((N, 128, C), dtype=np.float32))}
def setup_inputs_big(rng):
    d = setup_inputs(rng)
    for k in ("x",): d[k] = (d[k].astype(np.float32) * 1048576.0).astype(d[k].dtype)
    return d
def setup_inputs_small(rng):
    d = setup_inputs(rng)
    for k in ("x",): d[k] = (d[k].astype(np.float32) * (1 / 1048576.0)).astype(d[k].dtype)
    return d
def setup_inputs_mixed(rng):
    d = setup_inputs(rng)
    f = (10.0 ** rng.uniform(-3, 3, (1, 1, C))).astype(np.float32)
    for k in ("x",): d[k] = (d[k].astype(np.float32) * f).astype(d[k].dtype)
    return d
def reference(x):
    X = x.astype(np.float64)
    for _ in range(TIMES):
        X = X / X.sum(axis=2, keepdims=True)
        X = X / X.sum(axis=(0, 1), keepdims=True)
    return {"y": X.astype(np.float32)}

@@ -1,0 +1,121 @@
+from concourse.bass import DstId, RemoteDMATransfer
+from concourse.mybir import AluOpType, AxisListType, ActivationFunctionType
+
+F = "float32"
+SCRATCH = {
+    "xs": ("sbuf", [128, 256], F),
+    "xn": ("sbuf", [128, 256], F),
+    "z": ("sbuf", [128, 256], F),
+    "zs": ("sbuf", [128, 256], F),
+    "ys": ("sbuf", [128, 256], F),
+    "rs": ("sbuf", [128, 1], F),
+    "a": ("sbuf", [128, 1], F),
+    "ones": ("sbuf", [128, 128], F),
+    "e": ("sbuf", [128, 128], F),
+    "p": ("sbuf", [128, 128], F),
+    "mask": ("sbuf", [128, 4], F),
+    "land": ("sbuf", [128, 40], F),
+    "u": ("sbuf", [128, 16], F),
+    "v": ("sbuf", [128, 8], F),
+    "w": ("sbuf", [128, 8], F),
+    "b": ("sbuf", [128, 8], F),
+    "psp": ("psum", [128, 512], F),
+    "ps0": ("psum", [128, 512], F),
+    "ps1": ("psum", [128, 512], F),
+    "psw": ("psum", [128, 512], F),
+}
+SEMAPHORES = ["load", "ones", "mz", "mask", "e", "psp", "p", "rs", "a", "m0", "m1", "mine", "arr", "xn", "z",
+              "u", "v", "w", "t", "b", "q0", "q1", "q2", "q3", "back", "stored"]
+
+
+def rank_program(g, core, T, topo):
+    rank = T.rank_of(core)
+    if rank is None:
+        return
+    S = T.sem
+    n = len(T.cores)
+    V, PE, ACT, SY = g.vector, g.tensor, g.scalar, g.sync
+    mult, add = AluOpType.mult, AluOpType.add
+    copy = ActivationFunctionType.Copy
+
+    SY.dma_start(T.xs[:], T.x[:]).then_inc(S.load, 16)
+
+    V.memset(T.ones[0:32, :], 1.0).then_inc(S.ones, 1)
+    V.memset(T.mask[:], 0.0).then_inc(S.mz, 1)
+    V.wait_ge(S.mz, 1)
+    for k in range(4):
+        V.memset(T.mask[32 * k:32 * k + 32, k:k + 1], 1.0).then_inc(S.mask, 1)
+    V.wait_ge(S.mask, 4)
+    g.wait_ge(S.ones, 1)
+    g.affine_select(T.e[0:32, :], T.ones[0:32, :], [[0, 4], [-1, 32]], AluOpType.is_equal, 0.0, 0, 1).then_inc(S.e, 1)
+    PE.wait_ge(S.e, 1)
+    PE.matmul(T.psp[:, 0:128], T.e[0:32, :], T.e[0:32, :], True, True).then_inc(S.psp, 1)
+    ACT.wait_ge(S.psp, 1)
+    ACT.activation(T.p[:], T.psp[:, 0:128], copy).then_inc(S.p, 1)
+
+    V.wait_ge(S.load, 16)
+    V.tensor_reduce(T.rs[:], T.xs[:], AxisListType.X, add).then_inc(S.rs, 1)
+    V.wait_ge(S.rs, 1)
+    V.reciprocal(T.a[:], T.rs[:]).then_inc(S.a, 1)
+    PE.wait_ge(S.load, 16)
+    PE.wait_ge(S.a, 1)
+    PE.matmul(T.ps0[:, 0:1], T.xs[:, 0:128], T.a[:], True, True).then_inc(S.m0, 1)
+    PE.matmul(T.ps1[:, 0:1], T.xs[:, 128:256], T.a[:], True, True).then_inc(S.m1, 1)
+    own = T.land[:, 8 * rank:8 * rank + 8]
+    V.wait_ge(S.m0, 1)
+    V.tensor_scalar(T.land[:, 8 * rank:8 * rank + 4], T.mask[:], T.ps0[:, 0:1], None, mult).then_inc(S.mine, 1)
+    V.wait_ge(S.m1, 1)
+    V.tensor_scalar(T.land[:, 8 * rank + 4:8 * rank + 8], T.mask[:], T.ps1[:, 0:1], None, mult).then_inc(S.mine, 1)
+
+    others = [T.cores[(rank + k) % n] for k in range(1, n)]
+    engines = topo.mask(core, others[0])
+    for d in others:
+        assert topo.may_write(core, d)
+        engines &= topo.mask(core, d)
+    width = bin(engines).count("1")
+    ids = []
+    for d in others:
+        rid, pid, _se = topo.addr(d)
+        ids.append(DstId(rid=rid, pnc=pid))
+    g.wait_ge(S.mine, 2)
+    g.remote_dma_fused(
+        [RemoteDMATransfer(dst_ids=ids, dma_engine_mask=engines, remote_sem=S.arr,
+                           srcs=[own], dsts=[own for _ in others], alu_op=0)],
+        local_sem=S.arr)
+
+    ACT.wait_ge(S.load, 16)
+    ACT.wait_ge(S.a, 1)
+    ACT.activation(T.xn[:], T.xs[:], copy, scale=T.a[:, 0:1]).then_inc(S.xn, 1)
+    V.wait_ge(S.xn, 1)
+    V.transpose(T.z[:], T.xn[:]).then_inc(S.z, 1)
+    V.wait_ge(S.z, 1)
+
+    V.wait_ge(S.arr, width * n)
+    V.tensor_tensor(T.u[:], T.land[:, 0:16], T.land[:, 16:32], add).then_inc(S.u, 1)
+    V.wait_ge(S.u, 1)
+    V.tensor_tensor(T.v[:], T.u[:, 0:8], T.u[:, 8:16], add).then_inc(S.v, 1)
+    V.wait_ge(S.v, 1)
+    V.tensor_tensor(T.w[:], T.v[:], T.land[:, 32:40], add).then_inc(S.w, 1)
+    PE.wait_ge(S.p, 1)
+    PE.wait_ge(S.w, 1)
+    PE.matmul(T.psw[:, 0:8], T.p[:], T.w[:], True, True).then_inc(S.t, 1)
+    V.wait_ge(S.t, 1)
+    V.reciprocal(T.b[:], T.psw[:, 0:8]).then_inc(S.b, 1)
+
+    def blk(t, k):
+        return t[:, 32 * k:32 * k + 32]
+
+    V.wait_ge(S.b, 1)
+    for k in (0, 1):
+        V.tensor_scalar(blk(T.zs, k), blk(T.z, k), T.b[:, k:k + 1], None, mult).then_inc(S.q0, 1)
+    ACT.wait_ge(S.z, 1)
+    ACT.wait_ge(S.b, 1)
+    for k in range(2, 8):
+        ACT.activation(blk(T.zs, k), blk(T.z, k), copy, scale=T.b[:, k:k + 1]).then_inc(S["q%d" % (k // 2)], 1)
+    for h in range(4):
+        V.wait_ge(S["q%d" % h], 2)
+        V.transpose(T.ys[:, 64 * h:64 * h + 64], T.zs[:, 64 * h:64 * h + 64]).then_inc(S.back, 1)
+
+    SY.wait_ge(S.back, 4)
+    SY.dma_start(T.y[:], T.ys[:]).then_inc(S.stored, 16)
+    SY.wait_ge(S.stored, 16)

@@ -14,10 +14,10 @@ SCRATCH = {
     "e": ("sbuf", [128, 128], F),
     "p": ("sbuf", [128, 128], F),
     "mask": ("sbuf", [128, 4], F),
-    "land": ("sbuf", [128, 40], F),
+    "own": ("sbuf", [128, 8], F),
+    "land": ("sbuf", [128, 32], F),
     "u": ("sbuf", [128, 16], F),
     "v": ("sbuf", [128, 8], F),
-    "w": ("sbuf", [128, 8], F),
     "b": ("sbuf", [128, 8], F),
     "psp": ("psum", [128, 512], F),
     "ps0": ("psum", [128, 512], F),
@@ -25,7 +25,7 @@ SCRATCH = {
     "psw": ("psum", [128, 512], F),
 }
 SEMAPHORES = ["load", "ones", "mz", "mask", "e", "psp", "p", "rs", "a", "m0", "m1", "mine", "arr", "xn", "z",
-              "u", "v", "w", "t", "b", "q0", "q1", "q2", "q3", "back", "stored"]
+              "u", "v", "t", "b", "q0", "q1", "q2", "q3", "back0", "back1", "stored"]
 
 
 def rank_program(g, core, T, topo):
@@ -61,13 +61,13 @@ def rank_program(g, core, T, topo):
     PE.wait_ge(S.a, 1)
     PE.matmul(T.ps0[:, 0:1], T.xs[:, 0:128], T.a[:], True, True).then_inc(S.m0, 1)
     PE.matmul(T.ps1[:, 0:1], T.xs[:, 128:256], T.a[:], True, True).then_inc(S.m1, 1)
-    own = T.land[:, 8 * rank:8 * rank + 8]
     V.wait_ge(S.m0, 1)
-    V.tensor_scalar(T.land[:, 8 * rank:8 * rank + 4], T.mask[:], T.ps0[:, 0:1], None, mult).then_inc(S.mine, 1)
+    V.tensor_scalar(T.own[:, 0:4], T.mask[:], T.ps0[:, 0:1], None, mult).then_inc(S.mine, 1)
     V.wait_ge(S.m1, 1)
-    V.tensor_scalar(T.land[:, 8 * rank + 4:8 * rank + 8], T.mask[:], T.ps1[:, 0:1], None, mult).then_inc(S.mine, 1)
+    V.tensor_scalar(T.own[:, 4:8], T.mask[:], T.ps1[:, 0:1], None, mult).then_inc(S.mine, 1)
 
-    others = [T.cores[(rank + k) % n] for k in range(1, n)]
+    steps = list(range(1, n))
+    others = [T.cores[(rank + k) % n] for k in steps]
     engines = topo.mask(core, others[0])
     for d in others:
         assert topo.may_write(core, d)
@@ -80,9 +80,12 @@ def rank_program(g, core, T, topo):
     g.wait_ge(S.mine, 2)
     g.remote_dma_fused(
         [RemoteDMATransfer(dst_ids=ids, dma_engine_mask=engines, remote_sem=S.arr,
-                           srcs=[own], dsts=[own for _ in others], alu_op=0)],
+                           srcs=[T.own[:]], dsts=[T.land[:, 8 * (n - 1 - k):8 * (n - k)] for k in steps], alu_op=0)],
         local_sem=S.arr)
 
+    PE.wait_ge(S.p, 1)
+    PE.wait_ge(S.mine, 2)
+    PE.matmul(T.psw[:, 0:8], T.p[:], T.own[:], True, False)
     ACT.wait_ge(S.load, 16)
     ACT.wait_ge(S.a, 1)
     ACT.activation(T.xn[:], T.xs[:], copy, scale=T.a[:, 0:1]).then_inc(S.xn, 1)
@@ -94,11 +97,8 @@ def rank_program(g, core, T, topo):
     V.tensor_tensor(T.u[:], T.land[:, 0:16], T.land[:, 16:32], add).then_inc(S.u, 1)
     V.wait_ge(S.u, 1)
     V.tensor_tensor(T.v[:], T.u[:, 0:8], T.u[:, 8:16], add).then_inc(S.v, 1)
-    V.wait_ge(S.v, 1)
-    V.tensor_tensor(T.w[:], T.v[:], T.land[:, 32:40], add).then_inc(S.w, 1)
-    PE.wait_ge(S.p, 1)
-    PE.wait_ge(S.w, 1)
-    PE.matmul(T.psw[:, 0:8], T.p[:], T.w[:], True, True).then_inc(S.t, 1)
+    PE.wait_ge(S.v, 1)
+    PE.matmul(T.psw[:, 0:8], T.p[:], T.v[:], False, True).then_inc(S.t, 1)
     V.wait_ge(S.t, 1)
     V.reciprocal(T.b[:], T.psw[:, 0:8]).then_inc(S.b, 1)
 
@@ -106,16 +106,17 @@ def rank_program(g, core, T, topo):
         return t[:, 32 * k:32 * k + 32]
 
     V.wait_ge(S.b, 1)
-    for k in (0, 1):
-        V.tensor_scalar(blk(T.zs, k), blk(T.z, k), T.b[:, k:k + 1], None, mult).then_inc(S.q0, 1)
+    V.tensor_scalar(blk(T.zs, 0), blk(T.z, 0), T.b[:, 0:1], None, mult).then_inc(S.q0, 1)
     ACT.wait_ge(S.z, 1)
     ACT.wait_ge(S.b, 1)
-    for k in range(2, 8):
+    for k in range(1, 8):
         ACT.activation(blk(T.zs, k), blk(T.z, k), copy, scale=T.b[:, k:k + 1]).then_inc(S["q%d" % (k // 2)], 1)
     for h in range(4):
         V.wait_ge(S["q%d" % h], 2)
-        V.transpose(T.ys[:, 64 * h:64 * h + 64], T.zs[:, 64 * h:64 * h + 64]).then_inc(S.back, 1)
+        V.transpose(T.ys[:, 64 * h:64 * h + 64], T.zs[:, 64 * h:64 * h + 64]).then_inc(S["back%d" % (h // 2)], 1)
 
-    SY.wait_ge(S.back, 4)
-    SY.dma_start(T.y[:], T.ys[:]).then_inc(S.stored, 16)
-    SY.wait_ge(S.stored, 16)
+    SY.wait_ge(S.back0, 2)
+    SY.dma_start(T.y[:, 0:128], T.ys[:, 0:128]).then_inc(S.stored, 16)
+    SY.wait_ge(S.back1, 2)
+    SY.dma_start(T.y[:, 128:256], T.ys[:, 128:256]).then_inc(S.stored, 16)
+    SY.wait_ge(S.stored, 32)

@@ -16,16 +16,16 @@ SCRATCH = {
     "mask": ("sbuf", [128, 4], F),
     "own": ("sbuf", [128, 8], F),
     "land": ("sbuf", [128, 32], F),
-    "u": ("sbuf", [128, 16], F),
-    "v": ("sbuf", [128, 8], F),
+    "ev": ("sbuf", [128, 8], F),
+    "lv": ("sbuf", [128, 8], F),
     "b": ("sbuf", [128, 8], F),
     "psp": ("psum", [128, 512], F),
     "ps0": ("psum", [128, 512], F),
     "ps1": ("psum", [128, 512], F),
     "psw": ("psum", [128, 512], F),
 }
-SEMAPHORES = ["load", "ones", "mz", "mask", "e", "psp", "p", "rs", "a", "m0", "m1", "mine", "arr", "xn", "z",
-              "u", "v", "t", "b", "q0", "q1", "q2", "q3", "back0", "back1", "stored"]
+SEMAPHORES = ["load", "ones", "mz", "mask", "e", "psp", "p", "rs", "a", "m0", "m1", "mine", "arre", "arrl", "xn", "z",
+              "se", "sl", "t", "b", "q0", "q1", "q2", "q3", "back0", "back1", "stored"]
 
 
 def rank_program(g, core, T, topo):
@@ -67,21 +67,26 @@ def rank_program(g, core, T, topo):
     V.tensor_scalar(T.own[:, 4:8], T.mask[:], T.ps1[:, 0:1], None, mult).then_inc(S.mine, 1)
 
     steps = list(range(1, n))
-    others = [T.cores[(rank + k) % n] for k in steps]
-    engines = topo.mask(core, others[0])
-    for d in others:
+    engines = topo.mask(core, T.cores[(rank + 1) % n])
+    for k in steps:
+        d = T.cores[(rank + k) % n]
         assert topo.may_write(core, d)
         engines &= topo.mask(core, d)
     width = bin(engines).count("1")
-    ids = []
-    for d in others:
-        rid, pid, _se = topo.addr(d)
-        ids.append(DstId(rid=rid, pnc=pid))
+
+    def send(ks, sem):
+        ids = []
+        for k in ks:
+            rid, pid, _se = topo.addr(T.cores[(rank + k) % n])
+            ids.append(DstId(rid=rid, pnc=pid))
+        g.remote_dma_fused(
+            [RemoteDMATransfer(dst_ids=ids, dma_engine_mask=engines, remote_sem=sem,
+                               srcs=[T.own[:]], dsts=[T.land[:, 8 * (n - 1 - k):8 * (n - k)] for k in ks], alu_op=0)],
+            local_sem=sem)
+
     g.wait_ge(S.mine, 2)
-    g.remote_dma_fused(
-        [RemoteDMATransfer(dst_ids=ids, dma_engine_mask=engines, remote_sem=S.arr,
-                           srcs=[T.own[:]], dsts=[T.land[:, 8 * (n - 1 - k):8 * (n - k)] for k in steps], alu_op=0)],
-        local_sem=S.arr)
+    send(steps[:2], S.arre)
+    send(steps[2:], S.arrl)
 
     PE.wait_ge(S.p, 1)
     PE.wait_ge(S.mine, 2)
@@ -93,24 +98,30 @@ def rank_program(g, core, T, topo):
     V.transpose(T.z[:], T.xn[:]).then_inc(S.z, 1)
     V.wait_ge(S.z, 1)
 
-    V.wait_ge(S.arr, width * n)
-    V.tensor_tensor(T.u[:], T.land[:, 0:16], T.land[:, 16:32], add).then_inc(S.u, 1)
-    V.wait_ge(S.u, 1)
-    V.tensor_tensor(T.v[:], T.u[:, 0:8], T.u[:, 8:16], add).then_inc(S.v, 1)
-    PE.wait_ge(S.v, 1)
-    PE.matmul(T.psw[:, 0:8], T.p[:], T.v[:], False, True).then_inc(S.t, 1)
+    V.wait_ge(S.arre, width * 3)
+    V.tensor_tensor(T.ev[:], T.land[:, 16:24], T.land[:, 24:32], add).then_inc(S.se, 1)
+    PE.wait_ge(S.se, 1)
+    PE.matmul(T.psw[:, 0:8], T.p[:], T.ev[:], False, False)
+
+    V.wait_ge(S.arrl, width * 3)
+    V.tensor_tensor(T.lv[:], T.land[:, 0:8], T.land[:, 8:16], add).then_inc(S.sl, 1)
+    PE.wait_ge(S.sl, 1)
+    PE.matmul(T.psw[:, 0:8], T.p[:], T.lv[:], False, True).then_inc(S.t, 1)
     V.wait_ge(S.t, 1)
     V.reciprocal(T.b[:], T.psw[:, 0:8]).then_inc(S.b, 1)
 
     def blk(t, k):
         return t[:, 32 * k:32 * k + 32]
 
+    by_vector = (0, 2)
     V.wait_ge(S.b, 1)
-    V.tensor_scalar(blk(T.zs, 0), blk(T.z, 0), T.b[:, 0:1], None, mult).then_inc(S.q0, 1)
+    for k in by_vector:
+        V.tensor_scalar(blk(T.zs, k), blk(T.z, k), T.b[:, k:k + 1], None, mult).then_inc(S["q%d" % (k // 2)], 1)
     ACT.wait_ge(S.z, 1)
     ACT.wait_ge(S.b, 1)
-    for k in range(1, 8):
-        ACT.activation(blk(T.zs, k), blk(T.z, k), copy, scale=T.b[:, k:k + 1]).then_inc(S["q%d" % (k // 2)], 1)
+    for k in range(8):
+        if k not in by_vector:
+            ACT.activation(blk(T.zs, k), blk(T.z, k), copy, scale=T.b[:, k:k + 1]).then_inc(S["q%d" % (k // 2)], 1)
     for h in range(4):
         V.wait_ge(S["q%d" % h], 2)
         V.transpose(T.ys[:, 64 * h:64 * h + 64], T.zs[:, 64 * h:64 * h + 64]).then_inc(S["back%d" % (h // 2)], 1)

@@ -8,7 +8,7 @@ SCRATCH = {
     "z": ("sbuf", [128, 256], F),
     "zs": ("sbuf", [128, 256], F),
     "ys": ("sbuf", [128, 256], F),
-    "rs": ("sbuf", [128, 1], F),
+    "run": ("sbuf", [128, 128], F),
     "a": ("sbuf", [128, 1], F),
     "ones": ("sbuf", [128, 128], F),
     "e": ("sbuf", [128, 128], F),
@@ -16,16 +16,14 @@ SCRATCH = {
     "mask": ("sbuf", [128, 4], F),
     "own": ("sbuf", [128, 8], F),
     "land": ("sbuf", [128, 32], F),
-    "ev": ("sbuf", [128, 8], F),
-    "lv": ("sbuf", [128, 8], F),
     "b": ("sbuf", [128, 8], F),
     "psp": ("psum", [128, 512], F),
     "ps0": ("psum", [128, 512], F),
     "ps1": ("psum", [128, 512], F),
     "psw": ("psum", [128, 512], F),
 }
-SEMAPHORES = ["load", "ones", "mz", "mask", "e", "psp", "p", "rs", "a", "m0", "m1", "mine", "arre", "arrl", "xn", "z",
-              "se", "sl", "t", "b", "q0", "q1", "q2", "q3", "back0", "back1", "stored"]
+SEMAPHORES = ["load", "ones", "mz", "mask", "e", "psp", "p", "rs", "a", "m0", "m1", "mine", "arr1", "arr2", "arr3",
+              "arr4", "sent", "xn", "z", "t", "b", "q0", "q1", "q2", "q3", "back0", "back1", "stored0", "stored1"]
 
 
 def rank_program(g, core, T, topo):
@@ -54,9 +52,9 @@ def rank_program(g, core, T, topo):
     ACT.activation(T.p[:], T.psp[:, 0:128], copy).then_inc(S.p, 1)
 
     V.wait_ge(S.load, 16)
-    V.tensor_reduce(T.rs[:], T.xs[:], AxisListType.X, add).then_inc(S.rs, 1)
+    V.tensor_tensor_scan(T.run[:], T.xs[:, 0:128], T.xs[:, 128:256], 0.0, add, add).then_inc(S.rs, 1)
     V.wait_ge(S.rs, 1)
-    V.reciprocal(T.a[:], T.rs[:]).then_inc(S.a, 1)
+    V.reciprocal(T.a[:], T.run[:, 127:128]).then_inc(S.a, 1)
     PE.wait_ge(S.load, 16)
     PE.wait_ge(S.a, 1)
     PE.matmul(T.ps0[:, 0:1], T.xs[:, 0:128], T.a[:], True, True).then_inc(S.m0, 1)
@@ -74,23 +72,15 @@ def rank_program(g, core, T, topo):
         engines &= topo.mask(core, d)
     width = bin(engines).count("1")
 
-    def send(ks, sem):
-        ids = []
-        for k in ks:
-            rid, pid, _se = topo.addr(T.cores[(rank + k) % n])
-            ids.append(DstId(rid=rid, pnc=pid))
-        g.remote_dma_fused(
-            [RemoteDMATransfer(dst_ids=ids, dma_engine_mask=engines, remote_sem=sem,
-                               srcs=[T.own[:]], dsts=[T.land[:, 8 * (n - 1 - k):8 * (n - k)] for k in ks], alu_op=0)],
-            local_sem=sem)
-
     g.wait_ge(S.mine, 2)
-    send(steps[:2], S.arre)
-    send(steps[2:], S.arrl)
+    for k in steps:
+        rid, pid, _se = topo.addr(T.cores[(rank + k) % n])
+        g.remote_dma_fused(
+            [RemoteDMATransfer(dst_ids=[DstId(rid=rid, pnc=pid)], dma_engine_mask=engines,
+                               remote_sem=S["arr%d" % k], srcs=[T.own[:]],
+                               dsts=[T.land[:, 8 * (k - 1):8 * k]], alu_op=0)],
+            local_sem=S.sent)
 
-    PE.wait_ge(S.p, 1)
-    PE.wait_ge(S.mine, 2)
-    PE.matmul(T.psw[:, 0:8], T.p[:], T.own[:], True, False)
     ACT.wait_ge(S.load, 16)
     ACT.wait_ge(S.a, 1)
     ACT.activation(T.xn[:], T.xs[:], copy, scale=T.a[:, 0:1]).then_inc(S.xn, 1)
@@ -98,22 +88,21 @@ def rank_program(g, core, T, topo):
     V.transpose(T.z[:], T.xn[:]).then_inc(S.z, 1)
     V.wait_ge(S.z, 1)
 
-    V.wait_ge(S.arre, width * 3)
-    V.tensor_tensor(T.ev[:], T.land[:, 16:24], T.land[:, 24:32], add).then_inc(S.se, 1)
-    PE.wait_ge(S.se, 1)
-    PE.matmul(T.psw[:, 0:8], T.p[:], T.ev[:], False, False)
-
-    V.wait_ge(S.arrl, width * 3)
-    V.tensor_tensor(T.lv[:], T.land[:, 0:8], T.land[:, 8:16], add).then_inc(S.sl, 1)
-    PE.wait_ge(S.sl, 1)
-    PE.matmul(T.psw[:, 0:8], T.p[:], T.lv[:], False, True).then_inc(S.t, 1)
+    PE.wait_ge(S.p, 1)
+    PE.wait_ge(S.mine, 2)
+    PE.matmul(T.psw[:, 0:8], T.p[:], T.own[:], True, False)
+    for k in steps:
+        PE.wait_ge(S["arr%d" % k], width)
+        mm = PE.matmul(T.psw[:, 0:8], T.p[:], T.land[:, 8 * (k - 1):8 * k], False, k == steps[-1])
+        if k == steps[-1]:
+            mm.then_inc(S.t, 1)
     V.wait_ge(S.t, 1)
     V.reciprocal(T.b[:], T.psw[:, 0:8]).then_inc(S.b, 1)
 
     def blk(t, k):
         return t[:, 32 * k:32 * k + 32]
 
-    by_vector = (0, 2)
+    by_vector = (0, 2, 4)
     V.wait_ge(S.b, 1)
     for k in by_vector:
         V.tensor_scalar(blk(T.zs, k), blk(T.z, k), T.b[:, k:k + 1], None, mult).then_inc(S["q%d" % (k // 2)], 1)
@@ -127,7 +116,9 @@ def rank_program(g, core, T, topo):
         V.transpose(T.ys[:, 64 * h:64 * h + 64], T.zs[:, 64 * h:64 * h + 64]).then_inc(S["back%d" % (h // 2)], 1)
 
     SY.wait_ge(S.back0, 2)
-    SY.dma_start(T.y[:, 0:128], T.ys[:, 0:128]).then_inc(S.stored, 16)
-    SY.wait_ge(S.back1, 2)
-    SY.dma_start(T.y[:, 128:256], T.ys[:, 128:256]).then_inc(S.stored, 16)
-    SY.wait_ge(S.stored, 32)
+    SY.dma_start(T.y[:, 0:128], T.ys[:, 0:128]).then_inc(S.stored0, 16)
+    ACT.wait_ge(S.back1, 2)
+    ACT.dma_start(T.y[:, 128:256], T.ys[:, 128:256]).then_inc(S.stored1, 16)
+    g.wait_ge(S.sent, width * len(steps))
+    SY.wait_ge(S.stored0, 16)
+    ACT.wait_ge(S.stored1, 16)

from concourse.bass import DstId, RemoteDMATransfer
from concourse.mybir import AluOpType, AxisListType, ActivationFunctionType

F = "float32"
SCRATCH = {
    "xs": ("sbuf", [128, 256], F),
    "xn": ("sbuf", [128, 256], F),
    "z": ("sbuf", [128, 256], F),
    "zs": ("sbuf", [128, 256], F),
    "ys": ("sbuf", [128, 256], F),
    "run": ("sbuf", [128, 128], F),
    "a": ("sbuf", [128, 1], F),
    "ones": ("sbuf", [128, 128], F),
    "e": ("sbuf", [128, 128], F),
    "p": ("sbuf", [128, 128], F),
    "mask": ("sbuf", [128, 4], F),
    "own": ("sbuf", [128, 8], F),
    "land": ("sbuf", [128, 32], F),
    "b": ("sbuf", [128, 8], F),
    "psp": ("psum", [128, 512], F),
    "ps0": ("psum", [128, 512], F),
    "ps1": ("psum", [128, 512], F),
    "psw": ("psum", [128, 512], F),
}
SEMAPHORES = ["load", "ones", "mz", "mask", "e", "psp", "p", "rs", "a", "m0", "m1", "mine", "arr1", "arr2", "arr3",
              "arr4", "sent", "xn", "z", "t", "b", "q0", "q1", "q2", "q3", "back0", "back1", "stored0", "stored1"]


def rank_program(g, core, T, topo):
    rank = T.rank_of(core)
    if rank is None:
        return
    S = T.sem
    n = len(T.cores)
    V, PE, ACT, SY = g.vector, g.tensor, g.scalar, g.sync
    mult, add = AluOpType.mult, AluOpType.add
    copy = ActivationFunctionType.Copy

    SY.dma_start(T.xs[:], T.x[:]).then_inc(S.load, 16)

    V.memset(T.ones[0:32, :], 1.0).then_inc(S.ones, 1)
    V.memset(T.mask[:], 0.0).then_inc(S.mz, 1)
    V.wait_ge(S.mz, 1)
    for k in range(4):
        V.memset(T.mask[32 * k:32 * k + 32, k:k + 1], 1.0).then_inc(S.mask, 1)
    V.wait_ge(S.mask, 4)
    g.wait_ge(S.ones, 1)
    g.affine_select(T.e[0:32, :], T.ones[0:32, :], [[0, 4], [-1, 32]], AluOpType.is_equal, 0.0, 0, 1).then_inc(S.e, 1)
    PE.wait_ge(S.e, 1)
    PE.matmul(T.psp[:, 0:128], T.e[0:32, :], T.e[0:32, :], True, True).then_inc(S.psp, 1)
    ACT.wait_ge(S.psp, 1)
    ACT.activation(T.p[:], T.psp[:, 0:128], copy).then_inc(S.p, 1)

    V.wait_ge(S.load, 16)
    V.tensor_tensor_scan(T.run[:], T.xs[:, 0:128], T.xs[:, 128:256], 0.0, add, add).then_inc(S.rs, 1)
    V.wait_ge(S.rs, 1)
    V.reciprocal(T.a[:], T.run[:, 127:128]).then_inc(S.a, 1)
    PE.wait_ge(S.load, 16)
    PE.wait_ge(S.a, 1)
    PE.matmul(T.ps0[:, 0:1], T.xs[:, 0:128], T.a[:], True, True).then_inc(S.m0, 1)
    PE.matmul(T.ps1[:, 0:1], T.xs[:, 128:256], T.a[:], True, True).then_inc(S.m1, 1)
    V.wait_ge(S.m0, 1)
    V.tensor_scalar(T.own[:, 0:4], T.mask[:], T.ps0[:, 0:1], None, mult).then_inc(S.mine, 1)
    V.wait_ge(S.m1, 1)
    V.tensor_scalar(T.own[:, 4:8], T.mask[:], T.ps1[:, 0:1], None, mult).then_inc(S.mine, 1)

    steps = list(range(1, n))
    engines = topo.mask(core, T.cores[(rank + 1) % n])
    for k in steps:
        d = T.cores[(rank + k) % n]
        assert topo.may_write(core, d)
        engines &= topo.mask(core, d)
    width = bin(engines).count("1")

    g.wait_ge(S.mine, 2)
    for k in steps:
        rid, pid, _se = topo.addr(T.cores[(rank + k) % n])
        g.remote_dma_fused(
            [RemoteDMATransfer(dst_ids=[DstId(rid=rid, pnc=pid)], dma_engine_mask=engines,
                               remote_sem=S["arr%d" % k], srcs=[T.own[:]],
                               dsts=[T.land[:, 8 * (k - 1):8 * k]], alu_op=0)],
            local_sem=S.sent)

    ACT.wait_ge(S.load, 16)
    ACT.wait_ge(S.a, 1)
    ACT.activation(T.xn[:], T.xs[:], copy, scale=T.a[:, 0:1]).then_inc(S.xn, 1)
    V.wait_ge(S.xn, 1)
    V.transpose(T.z[:], T.xn[:]).then_inc(S.z, 1)
    V.wait_ge(S.z, 1)

    PE.wait_ge(S.p, 1)
    PE.wait_ge(S.mine, 2)
    PE.matmul(T.psw[:, 0:8], T.p[:], T.own[:], True, False)
    for k in steps:
        PE.wait_ge(S["arr%d" % k], width)
        mm = PE.matmul(T.psw[:, 0:8], T.p[:], T.land[:, 8 * (k - 1):8 * k], False, k == steps[-1])
        if k == steps[-1]:
            mm.then_inc(S.t, 1)
    V.wait_ge(S.t, 1)
    V.reciprocal(T.b[:], T.psw[:, 0:8]).then_inc(S.b, 1)

    def blk(t, k):
        return t[:, 32 * k:32 * k + 32]

    by_vector = (0, 2, 4)
    V.wait_ge(S.b, 1)
    for k in by_vector:
        V.tensor_scalar(blk(T.zs, k), blk(T.z, k), T.b[:, k:k + 1], None, mult).then_inc(S["q%d" % (k // 2)], 1)
    ACT.wait_ge(S.z, 1)
    ACT.wait_ge(S.b, 1)
    for k in range(8):
        if k not in by_vector:
            ACT.activation(blk(T.zs, k), blk(T.z, k), copy, scale=T.b[:, k:k + 1]).then_inc(S["q%d" % (k // 2)], 1)
    for h in range(4):
        V.wait_ge(S["q%d" % h], 2)
        V.transpose(T.ys[:, 64 * h:64 * h + 64], T.zs[:, 64 * h:64 * h + 64]).then_inc(S["back%d" % (h // 2)], 1)

    SY.wait_ge(S.back0, 2)
    SY.dma_start(T.y[:, 0:128], T.ys[:, 0:128]).then_inc(S.stored0, 16)
    ACT.wait_ge(S.back1, 2)
    ACT.dma_start(T.y[:, 128:256], T.ys[:, 128:256]).then_inc(S.stored1, 16)
    g.wait_ge(S.sent, width * len(steps))
    SY.wait_ge(S.stored0, 16)
    ACT.wait_ge(S.stored1, 16)
